import numpy as np
import ml_dtypes


def mxq(x, axis, fmt="e4m3"):
    dtype, down = {"e4m3": (ml_dtypes.float8_e4m3fn, 7), "e5m2": (ml_dtypes.float8_e5m2, 14)}[fmt]
    v = np.moveaxis(np.asarray(x, np.float32).astype(ml_dtypes.bfloat16).astype(np.float64), axis, -1)
    blocks = v.reshape(v.shape[:-1] + (-1, 32))
    amax = np.abs(blocks).max(-1, keepdims=True)
    byte = np.maximum(np.where(amax > 0, np.frexp(amax)[1] - 1 + 127, 0) - down, 1)
    scale = np.exp2(byte - 127.0)
    codes = (blocks / scale).astype(np.float32).astype(dtype).astype(np.float64)
    return np.moveaxis((codes * scale).reshape(v.shape), -1, axis)


WIDE = False


def mx_kscale(k):
    if not WIDE:
        return np.ones(k)
    levels = np.array([10, -10, 5, -5, 0])
    if k % 512:
        return np.exp2(np.random.permutation(np.resize(levels, k // 32))).repeat(32)
    a = np.empty((k // 512, 16))
    for p in range(k // 512):
        a[p, :8] = np.random.permutation(np.resize(levels, 8))
        for g in range(8):
            far = levels[np.abs(levels - a[p, g]) >= 10]
            a[p, g + 8] = far[np.random.randint(len(far))]
    return np.exp2(a.ravel()).repeat(32)


BF16 = ml_dtypes.bfloat16


def bf(x):
    return np.asarray(x, np.float32).astype(BF16)


def f64(x):
    return np.asarray(x).astype(np.float64)


N, M, L = 128, 4096, 4096


def draw0():
    u, t = mx_kscale(M), mx_kscale(L)
    return {"s": bf(3.0 / np.sqrt(L) * np.random.standard_normal((N, L))),
            "z": bf(2.0 / np.sqrt(L) * np.random.standard_normal((M, L)) / u[:, None]),
            "kgain": bf(1.5 / np.sqrt(M) * np.random.standard_normal((N, M)) * u[None, :]),
            "g": bf((1.0 + 0.2 * np.random.standard_normal(L)) * t),
            "d": bf(np.random.uniform(0.5, 2.0, L) / (t * t)),
            "r": bf(np.random.uniform(1.0, 3.0, M) / (u * u))}


def weighted_gram(left, right):
    return left @ right.T


def core(s, z, kgain, g, d, r):
    k = f64(kgain)
    kq = mxq(k, 1, "e4m3")
    kz = kq @ mxq(f64(z), 0, "e4m3")
    w = (f64(s) - kz) * f64(g)[None, :]
    wd = w * f64(d)[None, :]
    j = weighted_gram(mxq(wd, 1, "e4m3"), mxq(w, 1, "e4m3"))
    kr = k * f64(r)[None, :]
    q = weighted_gram(mxq(kr, 1, "e4m3"), kq)
    return j + q


def e4m3fn_bytes(y):
    return np.clip(np.asarray(y, np.float64), -448.0, 448.0).astype(np.float32).astype(ml_dtypes.float8_e4m3fn).view(np.uint8)


def e4m3fn_values(b):
    return np.asarray(b, np.uint8).view(ml_dtypes.float8_e4m3fn).astype(np.float64)


def setup_inputs():
    d = draw0()
    x0 = np.asarray(d['z']).astype(np.float64)
    s = (np.max(np.abs(x0), axis=(1,), keepdims=True) / 448.0).astype(np.float32)
    out = {}
    for k, v in d.items():
        if k == 'z':
            out['z_bytes'] = e4m3fn_bytes(x0 / s.astype(np.float64))
            out['z_scale'] = s
        else:
            out[k] = v
    return out


def reference(s, z_bytes, z_scale, kgain, g, d, r):
    return core(s, e4m3fn_values(z_bytes) * z_scale.astype(np.float64), kgain, g, d, r)

@@ -1,0 +1,365 @@
+from contextlib import ExitStack
+
+import concourse.mybir as mybir
+from concourse.masks import make_identity
+
+N, M, L = 128, 4096, 4096
+FLOPS = 2 * N * M * L + 4 * N * N * L
+
+F32 = mybir.dt.float32
+BF16 = mybir.dt.bfloat16
+U32 = mybir.dt.uint32
+U8 = mybir.dt.uint8
+F8 = mybir.dt.float8_e4m3fn
+FP8X4 = mybir.dt.float8_e4m3fn_x4
+MULT = mybir.AluOpType.mult
+SUB = mybir.AluOpType.subtract
+COPY = mybir.ActivationFunctionType.Copy
+
+P = 128
+KP = M // 512
+CHUNKS = [512, 1024, 1024, 1024, 512]
+WMAX = 1024
+
+
+def tile_josephkalmanupdate_w_kernel(tc, s, z_bytes, z_scale, kgain, g, d, r, out):
+    nc = tc.nc
+    with ExitStack() as ctx:
+        keep = ctx.enter_context(tc.tile_pool(name="keep", bufs=1))
+        bpool = ctx.enter_context(tc.tile_pool(name="bpool", bufs=5))
+        work = ctx.enter_context(tc.tile_pool(name="work", bufs=3))
+        cpool = ctx.enter_context(tc.tile_pool(name="cpool", bufs=2))
+        epool = ctx.enter_context(tc.tile_pool(name="epool", bufs=2))
+        psum = ctx.enter_context(tc.psum_pool(name="psum", bufs=1))
+
+        units = []
+        l0 = 0
+        for c, w in enumerate(CHUNKS):
+            for gp in range(KP):
+                units.append((c, gp, l0, w))
+            l0 += w
+        nu = len(units)
+
+        ident = keep.tile([P, P], F32, name="ident")
+        identb = keep.tile([P, P], BF16, name="identb")
+        zs = keep.tile([P, KP, 4], F32, name="zs")
+        rt = keep.tile([P, KP, 4], BF16, name="rt")
+        gdraw = keep.tile([P, 512], BF16, name="gdraw")
+        gdperm = keep.tile([P, 4, P], BF16, name="gdperm")
+        gT = keep.tile([P, 8, 4], F32, name="gT")
+        dT = keep.tile([P, 8, 4], F32, name="dT")
+        gdT = keep.tile([P, 8, 4], F32, name="gdT")
+        kg = keep.tile([P, M], BF16, name="kg")
+        kT = keep.tile([P, KP, P * 4], BF16, name="kT", align_bytes=64)
+        krT = keep.tile([P, KP, P * 4], BF16, name="krT", align_bytes=64)
+        kq = keep.tile([P, KP, P], U32, name="kq", align_bytes=64)
+        kqs = keep.tile([P, KP, P], U8, name="kqs", align_bytes=64)
+        krq = keep.tile([P, KP, P], U32, name="krq", align_bytes=64)
+        krqs = keep.tile([P, KP, P], U8, name="krqs", align_bytes=64)
+        sraw = keep.tile([P, L], BF16, name="sraw")
+        sperm = keep.tile([P, 8, 4, P], BF16, name="sperm")
+        sT = keep.tile([P, 8, 4, P], BF16, name="sT")
+
+        qj = psum.tile([P, P], F32, name="qj", tag="qj", bufs=1)
+
+        zb = {}
+        planes = {}
+        il = {}
+        codes = {}
+        kz = {}
+        ep = {}
+
+        def load(u):
+            c, gp, lo, w = units[u]
+            t_ = bpool.tile([P, 4, WMAX], U8, name="zb", tag="zb", bufs=5)
+            nc.sync.dma_start(
+                out=t_[:, :, 0:w],
+                in_=z_bytes[512 * gp : 512 * (gp + 1), lo : lo + w].rearrange("(p t) w -> p t w", t=4),
+            )
+            zb[u] = t_
+
+        def widen(u, nv):
+            c, gp, lo, w = units[u]
+            p_ = work.tile([P, 4, w], BF16, name="planes", tag="planes%d" % w, bufs=3 if w == WMAX else 2, align_bytes=64)
+            planes[u] = p_
+            for t in range(4):
+                src = zb[u][:, t, 0:w].bitcast(F8)
+                sc = zs[:, gp, t : t + 1]
+                if t < nv:
+                    nc.vector.tensor_scalar(out=p_[:, t, :], in0=src, scalar1=sc, scalar2=None, op0=MULT)
+                else:
+                    nc.scalar.activation(out=p_[:, t, :], in_=src, func=COPY, scale=sc)
+
+        def inter(u):
+            c, gp, lo, w = units[u]
+            i_ = work.tile([P, 4 * WMAX], BF16, name="il", tag="il", bufs=2, align_bytes=64)
+            il[u] = i_
+            nc.vector.tensor_copy(
+                out=i_[:, 0 : 4 * w].rearrange("p (T A i t) -> p T A t i", T=4, i=4, t=4),
+                in_=planes[u][:].rearrange("p t (A T i) -> p T A t i", T=4, i=4),
+            )
+
+        def quant(u):
+            c, gp, lo, w = units[u]
+            if gp == 0:
+                codes[c] = (
+                    cpool.tile([P, KP, WMAX], U32, name="zc", tag="zc", bufs=2, align_bytes=64),
+                    cpool.tile([P, KP, WMAX], U8, name="zsc", tag="zsc", bufs=2, align_bytes=64),
+                )
+            cd, sc = codes[c]
+            nc.vector.quantize_mx(
+                out=cd[:, gp, 0:w].bitcast(FP8X4), scales=sc[:, gp, 0:w], in_=il[u][:, 0 : 4 * w]
+            )
+
+        def kzpass(c, h, T, gp, dst):
+            cd, sc = codes[c]
+            w = CHUNKS[c]
+            c0 = T * (w // 4) + 128 * h
+            nc.tensor.matmul_mx(
+                out=dst,
+                lhsT=cd[:, gp, c0 : c0 + 128].bitcast(FP8X4),
+                lhsT_scale=sc[:, gp, c0 : c0 + 128],
+                rhs=kq[:, gp, :].bitcast(FP8X4),
+                rhs_scale=kqs[:, gp, :],
+                start=(gp == 0),
+                stop=(gp == KP - 1),
+            )
+
+        def kzall(c):
+            for h in range(CHUNKS[c] // 512):
+                b_ = psum.tile([P, 4, P], F32, name="kz", tag="kz", bufs=3)
+                kz[(c, h)] = b_
+                for T in range(4):
+                    for gp in range(KP):
+                        kzpass(c, h, T, gp, b_[:, T, :])
+
+        def hh0(c):
+            return sum(CHUNKS[:c]) // 512
+
+        def e_alloc(c):
+            nh = CHUNKS[c] // 512
+            ep[c] = dict(
+                t1=epool.tile([P, 2, 512], F32, name="t1", tag="t1", bufs=2),
+                w=epool.tile([P, 2, 512], BF16, name="w", tag="w", bufs=2, align_bytes=64),
+                wd=epool.tile([P, 2, 512], BF16, name="wd", tag="wd", bufs=2, align_bytes=64),
+                wq=epool.tile([P, 2, P], U32, name="wq", tag="wq", bufs=2, align_bytes=64),
+                wqs=epool.tile([P, 2, P], U8, name="wqs", tag="wqs", bufs=2, align_bytes=64),
+                wdq=epool.tile([P, 2, P], U32, name="wdq", tag="wdq", bufs=2, align_bytes=64),
+                wdqs=epool.tile([P, 2, P], U8, name="wdqs", tag="wdqs", bufs=2, align_bytes=64),
+            )
+
+        def e_t1(c, h):
+            if h == 0:
+                e_alloc(c)
+            hh = hh0(c) + h
+            nc.vector.tensor_tensor(
+                out=ep[c]["t1"][:, h, :],
+                in0=sT[:, hh, :, :].rearrange("p T n -> p (T n)"),
+                in1=kz[(c, h)][:].rearrange("p T n -> p (T n)"),
+                op=SUB,
+            )
+
+        def e_mul(c, h, key, gain):
+            hh = hh0(c) + h
+            nc.vector.tensor_tensor(
+                out=ep[c][key][:, h, :].rearrange("p (n T) -> p n T", T=4),
+                in0=ep[c]["t1"][:, h, :].rearrange("p (T n) -> p n T", T=4),
+                in1=gain[:, hh, :].unsqueeze(1).to_broadcast([P, P, 4]),
+                op=MULT,
+            )
+
+        def e_q(c, key):
+            nh = CHUNKS[c] // 512
+            e = ep[c]
+            nc.vector.quantize_mx(
+                out=e[key + "q"][:, 0:nh, :].rearrange("p h n -> p (h n)").bitcast(FP8X4),
+                scales=e[key + "qs"][:, 0:nh, :].rearrange("p h n -> p (h n)"),
+                in_=e[key][:, 0:nh, :].rearrange("p h x -> p (h x)"),
+            )
+
+        def e_j(c):
+            e = ep[c]
+            for h in range(CHUNKS[c] // 512):
+                nc.tensor.matmul_mx(
+                    out=qj[:],
+                    lhsT=e["wdq"][:, h, :].bitcast(FP8X4),
+                    lhsT_scale=e["wdqs"][:, h, :],
+                    rhs=e["wq"][:, h, :].bitcast(FP8X4),
+                    rhs_scale=e["wqs"][:, h, :],
+                    start=False,
+                    stop=(hh0(c) + h == 7),
+                )
+
+        def tp_f32():
+            return psum.tile([P, 2, 2, P], F32, name="tp", tag="tp", bufs=4)
+
+        def k_turn(q):
+            ps = tp_f32()
+            words = kg[:].bitcast(F32)
+            for j in range(2):
+                for u in range(2):
+                    b0 = 256 * (2 * q + j)
+                    nc.tensor.transpose(ps[:, j, u, :], words[:, b0 + u : b0 + 256 : 2], ident[:])
+            nc.scalar.copy(
+                out=kT[:, 2 * q : 2 * q + 2, :].bitcast(F32).rearrange("p j (n u) -> p j n u", u=2),
+                in_=ps[:].rearrange("p j u n -> p j n u"),
+            )
+
+        def k_q(q):
+            a, b = 4 * q, 4 * q + 4
+            nc.vector.quantize_mx(
+                out=kq[:, a:b, :].rearrange("p g n -> p (g n)").bitcast(FP8X4),
+                scales=kqs[:, a:b, :].rearrange("p g n -> p (g n)"),
+                in_=kT[:, a:b, :].rearrange("p g x -> p (g x)"),
+            )
+
+        def kr_mul(q):
+            a, b = 4 * q, 4 * q + 4
+            nc.vector.tensor_tensor(
+                out=krT[:, a:b, :].rearrange("p g (n t) -> p g n t", t=4),
+                in0=kT[:, a:b, :].rearrange("p g (n t) -> p g n t", t=4),
+                in1=rt[:, a:b, :].unsqueeze(2).to_broadcast([P, 4, P, 4]),
+                op=MULT,
+            )
+
+        def kr_q(q):
+            a, b = 4 * q, 4 * q + 4
+            nc.vector.quantize_mx(
+                out=krq[:, a:b, :].rearrange("p g n -> p (g n)").bitcast(FP8X4),
+                scales=krqs[:, a:b, :].rearrange("p g n -> p (g n)"),
+                in_=krT[:, a:b, :].rearrange("p g x -> p (g x)"),
+            )
+
+        def q_all():
+            for gp in range(KP):
+                nc.tensor.matmul_mx(
+                    out=qj[:],
+                    lhsT=krq[:, gp, :].bitcast(FP8X4),
+                    lhsT_scale=krqs[:, gp, :],
+                    rhs=kq[:, gp, :].bitcast(FP8X4),
+                    rhs_scale=kqs[:, gp, :],
+                    start=(gp == 0),
+                    stop=False,
+                )
+
+        def s_perm(q):
+            nc.scalar.copy(
+                out=sperm[:, q, :, :].rearrange("p T (A i) -> p T A i", i=4),
+                in_=sraw[:, 512 * q : 512 * (q + 1)].rearrange("p (A T i) -> p T A i", T=4, i=4),
+            )
+
+        def s_turn(q):
+            ps = psum.tile([P, 4, P], BF16, name="tp", tag="tp", bufs=4)
+            for T in range(4):
+                nc.tensor.transpose(ps[:, T, :], sperm[:, q, T, :], identb[:])
+            nc.scalar.copy(out=sT[:, q, :, :], in_=ps[:])
+
+        def gd_prep():
+            nc.vector.tensor_copy(
+                out=gdperm[:].rearrange("p T (A i) -> p T A i", i=4),
+                in_=gdraw[:].rearrange("p (A T i) -> p T A i", T=4, i=4),
+            )
+            ps = psum.tile([P, 4, P], BF16, name="tp", tag="tp", bufs=4)
+            for T in range(4):
+                nc.tensor.transpose(ps[:, T, :], gdperm[:, T, :], identb[:])
+            nc.vector.tensor_copy(out=gT[:].rearrange("p h T -> p T h"), in_=ps[:, :, 0:8])
+            nc.vector.tensor_copy(out=dT[:].rearrange("p h T -> p T h"), in_=ps[:, :, 8:16])
+            nc.vector.tensor_tensor(out=gdT[:], in0=gT[:], in1=dT[:], op=MULT)
+
+        def vplanes(u):
+            if u == 0:
+                return 2
+            if u == 1:
+                return 2
+            if u >= 34:
+                return 0
+            return 1 if u % 4 == 0 else 0
+
+        tasks = {}
+
+        def at(step, fn, *args):
+            tasks.setdefault(step, []).append((fn, args))
+
+        at(1, k_turn, 0)
+        at(1, k_turn, 1)
+        at(2, k_turn, 2)
+        at(2, k_turn, 3)
+        at(2, gd_prep)
+        at(3, k_q, 0)
+        at(4, k_q, 1)
+        at(5, kr_mul, 0)
+        at(6, kr_mul, 1)
+        at(7, kr_q, 0)
+        at(8, kr_q, 1)
+        at(8, q_all)
+        step0 = 0
+        for c, w in enumerate(CHUNKS):
+            end = 8 * (c + 1) - 1
+            for h in range(w // 512):
+                at(end - 11 + h if c == len(CHUNKS) - 1 else end - 3 + h, s_perm, hh0(c) + h)
+                at(end - 10 + h if c == len(CHUNKS) - 1 else end - 2 + h, s_turn, hh0(c) + h)
+            if c < len(CHUNKS) - 1:
+                k = end + 3
+                for h in range(w // 512):
+                    at(k + h, e_t1, c, h)
+                for h in range(w // 512):
+                    at(k + 2, e_mul, c, h, "w", gT)
+                for h in range(w // 512):
+                    at(k + 3, e_mul, c, h, "wd", gdT)
+                at(k + 3, e_q, c, "w")
+                at(k + 4, e_q, c, "wd")
+                at(k + 4, e_j, c)
+
+        with tc.manual_schedule():
+            nc.scalar.dma_start(out=zs[:], in_=z_scale.rearrange("(g p t) o -> p g (t o)", p=P, t=4))
+            load(0)
+            load(1)
+            nc.sync.dma_start(out=kg[:], in_=kgain)
+            nc.gpsimd.memset(gdraw[:], 0.0)
+            make_identity(nc, ident[:])
+            nc.gpsimd.tensor_copy(out=identb[:], in_=ident[:])
+            load(2)
+            nc.sync.dma_start(out=rt[:], in_=r.rearrange("(g p t) -> p g t", p=P, t=4))
+            nc.sync.dma_start(out=gdraw[0:8, :], in_=g.rearrange("(h x) -> h x", h=8))
+            nc.sync.dma_start(out=gdraw[8:16, :], in_=d.rearrange("(h x) -> h x", h=8))
+            load(3)
+            nc.sync.dma_start(out=sraw[:], in_=s)
+
+            widen(0, vplanes(0))
+            widen(1, vplanes(1))
+            inter(0)
+            last = len(CHUNKS) - 1
+            fin = []
+            for u in range(nu):
+                if 4 <= u + 4 < nu:
+                    load(u + 4)
+                if u + 2 < nu:
+                    widen(u + 2, vplanes(u + 2))
+                if u + 1 < nu:
+                    inter(u + 1)
+                for fn, args in tasks.get(u, []):
+                    fn(*args)
+                quant(u)
+                c, gp, lo, w = units[u]
+                if c < last:
+                    if gp == KP - 1:
+                        kzall(c)
+                else:
+                    if gp == 0:
+                        for T in range(4):
+                            fin.append(psum.tile([P, P], F32, name="tp", tag="tp", bufs=4))
+                    for T in range(4):
+                        kzpass(c, 0, T, gp, fin[T][:])
+            e_alloc(last)
+            for T in range(4):
+                nc.vector.tensor_tensor(
+                    out=ep[last]["t1"][:, 0, 128 * T : 128 * (T + 1)], in0=sT[:, 7, T, :], in1=fin[T][:], op=SUB
+                )
+            e_mul(last, 0, "wd", gdT)
+            e_mul(last, 0, "w", gT)
+            e_q(last, "wd")
+            e_q(last, "w")
+            e_j(last)
+            res = epool.tile([P, P], F32, name="res", tag="res", bufs=1)
+            nc.vector.tensor_copy(out=res[:], in_=qj[:])
+            nc.sync.dma_start(out=out, in_=res[:])

@@ -57,7 +57,7 @@ def tile_josephkalmanupdate_w_kernel(tc, s, z_bytes, z_scale, kgain, g, d, r, ou
         krq = keep.tile([P, KP, P], U32, name="krq", align_bytes=64)
         krqs = keep.tile([P, KP, P], U8, name="krqs", align_bytes=64)
         sraw = keep.tile([P, L], BF16, name="sraw")
-        sperm = keep.tile([P, 8, 4, P], BF16, name="sperm")
+        sperm = {}
         sT = keep.tile([P, 8, 4, P], BF16, name="sT")
 
         qj = psum.tile([P, P], F32, name="qj", tag="qj", bufs=1)
@@ -78,30 +78,51 @@ def tile_josephkalmanupdate_w_kernel(tc, s, z_bytes, z_scale, kgain, g, d, r, ou
             )
             zb[u] = t_
 
-        def widen(u, nv):
+        def widen_e(u):
             c, gp, lo, w = units[u]
-            p_ = work.tile([P, 4, w], BF16, name="planes", tag="planes%d" % w, bufs=3 if w == WMAX else 2, align_bytes=64)
+            p_ = work.tile([P, 2, WMAX * 2], BF16, name="pairs", tag="pairs", bufs=2, align_bytes=64)
             planes[u] = p_
             for t in range(4):
-                src = zb[u][:, t, 0:w].bitcast(F8)
-                sc = zs[:, gp, t : t + 1]
-                if t < nv:
-                    nc.vector.tensor_scalar(out=p_[:, t, :], in0=src, scalar1=sc, scalar2=None, op0=MULT)
-                else:
-                    nc.scalar.activation(out=p_[:, t, :], in_=src, func=COPY, scale=sc)
+                nc.vector.tensor_scalar(
+                    out=p_[:, t // 2, 0 : 2 * w].rearrange("p (T A i e) -> p e A T i", T=4, i=4, e=2)[:, t % 2],
+                    in0=zb[u][:, t, 0:w].bitcast(F8).rearrange("p (A T i) -> p A T i", T=4, i=4),
+                    scalar1=zs[:, gp, t : t + 1],
+                    scalar2=None,
+                    op0=MULT,
+                )
 
-        def inter(u):
+        def il_alloc(u):
+            il[u] = work.tile([P, 4 * WMAX], BF16, name="il", tag="il", bufs=4, align_bytes=64)
+
+        def word(u, eng, lo=0, hi=None):
+            c, gp, l_, w = units[u]
+            hi = w if hi is None else hi
+            f = nc.scalar.copy if eng == "S" else nc.vector.tensor_copy
+            f(
+                out=il[u][:, 4 * lo : 4 * hi].bitcast(F32).rearrange("p (c u) -> p c u", u=2),
+                in_=planes[u][:].rearrange("p u x -> p (u x)").bitcast(F32).rearrange("p (u c) -> p c u", u=2)[:, lo:hi, :],
+            )
+
+        def d_widen(u, t):
             c, gp, lo, w = units[u]
-            i_ = work.tile([P, 4 * WMAX], BF16, name="il", tag="il", bufs=2, align_bytes=64)
-            il[u] = i_
-            nc.vector.tensor_copy(
-                out=i_[:, 0 : 4 * w].rearrange("p (T A i t) -> p T A t i", T=4, i=4, t=4),
-                in_=planes[u][:].rearrange("p t (A T i) -> p T A t i", T=4, i=4),
+            if t == 0:
+                planes[u] = work.tile([P, 4, WMAX], BF16, name="planes", tag="planes", bufs=2, align_bytes=64)
+            nc.scalar.activation(
+                out=planes[u][:, t, 0:w], in_=zb[u][:, t, 0:w].bitcast(F8), func=COPY, scale=zs[:, gp, t : t + 1]
+            )
+
+        def d_inter(u, T):
+            c, gp, lo, w = units[u]
+            if T == 0:
+                il_alloc(u)
+            nc.scalar.copy(
+                out=il[u][:, T * w : (T + 1) * w].rearrange("p (A i t) -> p A t i", i=4, t=4),
+                in_=planes[u][:, :, 0:w].rearrange("p t (A T i) -> p T A t i", T=4, i=4)[:, T],
             )
 
         def quant(u):
             c, gp, lo, w = units[u]
-            if gp == 0:
+            if c not in codes:
                 codes[c] = (
                     cpool.tile([P, KP, WMAX], U32, name="zc", tag="zc", bufs=2, align_bytes=64),
                     cpool.tile([P, KP, WMAX], U8, name="zsc", tag="zsc", bufs=2, align_bytes=64),
@@ -111,7 +132,7 @@ def tile_josephkalmanupdate_w_kernel(tc, s, z_bytes, z_scale, kgain, g, d, r, ou
                 out=cd[:, gp, 0:w].bitcast(FP8X4), scales=sc[:, gp, 0:w], in_=il[u][:, 0 : 4 * w]
             )
 
-        def kzpass(c, h, T, gp, dst):
+        def kzpass(c, h, T, gp, dst, first=0, final=KP - 1):
             cd, sc = codes[c]
             w = CHUNKS[c]
             c0 = T * (w // 4) + 128 * h
@@ -121,8 +142,8 @@ def tile_josephkalmanupdate_w_kernel(tc, s, z_bytes, z_scale, kgain, g, d, r, ou
                 lhsT_scale=sc[:, gp, c0 : c0 + 128],
                 rhs=kq[:, gp, :].bitcast(FP8X4),
                 rhs_scale=kqs[:, gp, :],
-                start=(gp == 0),
-                stop=(gp == KP - 1),
+                start=(gp == first),
+                stop=(gp == final),
             )
 
         def kzall(c):
@@ -139,9 +160,9 @@ def tile_josephkalmanupdate_w_kernel(tc, s, z_bytes, z_scale, kgain, g, d, r, ou
         def e_alloc(c):
             nh = CHUNKS[c] // 512
             ep[c] = dict(
-                t1=epool.tile([P, 2, 512], F32, name="t1", tag="t1", bufs=2),
-                w=epool.tile([P, 2, 512], BF16, name="w", tag="w", bufs=2, align_bytes=64),
-                wd=epool.tile([P, 2, 512], BF16, name="wd", tag="wd", bufs=2, align_bytes=64),
+                t1=epool.tile([P, 2, 512], F32, name="t1", tag="t1", bufs=1),
+                w=epool.tile([P, 2, 512], BF16, name="w", tag="w", bufs=1, align_bytes=64),
+                wd=epool.tile([P, 2, 512], BF16, name="wd", tag="wd", bufs=1, align_bytes=64),
                 wq=epool.tile([P, 2, P], U32, name="wq", tag="wq", bufs=2, align_bytes=64),
                 wqs=epool.tile([P, 2, P], U8, name="wqs", tag="wqs", bufs=2, align_bytes=64),
                 wdq=epool.tile([P, 2, P], U32, name="wdq", tag="wdq", bufs=2, align_bytes=64),
@@ -153,18 +174,18 @@ def tile_josephkalmanupdate_w_kernel(tc, s, z_bytes, z_scale, kgain, g, d, r, ou
                 e_alloc(c)
             hh = hh0(c) + h
             nc.vector.tensor_tensor(
-                out=ep[c]["t1"][:, h, :],
-                in0=sT[:, hh, :, :].rearrange("p T n -> p (T n)"),
-                in1=kz[(c, h)][:].rearrange("p T n -> p (T n)"),
+                out=ep[c]["t1"][:, h, :].rearrange("p (n T) -> p n T", T=4),
+                in0=sT[:, hh, :, :].rearrange("p T n -> p n T"),
+                in1=kz[(c, h)][:].rearrange("p T n -> p n T"),
                 op=SUB,
             )
 
-        def e_mul(c, h, key, gain):
-            hh = hh0(c) + h
+        def e_mul(c, key, gain):
+            nh = CHUNKS[c] // 512
             nc.vector.tensor_tensor(
-                out=ep[c][key][:, h, :].rearrange("p (n T) -> p n T", T=4),
-                in0=ep[c]["t1"][:, h, :].rearrange("p (T n) -> p n T", T=4),
-                in1=gain[:, hh, :].unsqueeze(1).to_broadcast([P, P, 4]),
+                out=ep[c][key][:, 0:nh, :].rearrange("p h (n T) -> p h n T", T=4),
+                in0=ep[c]["t1"][:, 0:nh, :].rearrange("p h (T n) -> p h n T" if c == len(CHUNKS) - 1 else "p h (n T) -> p h n T", T=4),
+                in1=gain[:, hh0(c) : hh0(c) + nh, :].unsqueeze(2).to_broadcast([P, nh, P, 4]),
                 op=MULT,
             )
 
@@ -243,15 +264,16 @@ def tile_josephkalmanupdate_w_kernel(tc, s, z_bytes, z_scale, kgain, g, d, r, ou
                 )
 
         def s_perm(q):
+            sperm[q] = epool.tile([P, 4, P], BF16, name="sperm", tag="sperm", bufs=2)
             nc.scalar.copy(
-                out=sperm[:, q, :, :].rearrange("p T (A i) -> p T A i", i=4),
+                out=sperm[q][:].rearrange("p T (A i) -> p T A i", i=4),
                 in_=sraw[:, 512 * q : 512 * (q + 1)].rearrange("p (A T i) -> p T A i", T=4, i=4),
             )
 
         def s_turn(q):
             ps = psum.tile([P, 4, P], BF16, name="tp", tag="tp", bufs=4)
             for T in range(4):
-                nc.tensor.transpose(ps[:, T, :], sperm[:, q, T, :], identb[:])
+                nc.tensor.transpose(ps[:, T, :], sperm[q][:, T, :], identb[:])
             nc.scalar.copy(out=sT[:, q, :, :], in_=ps[:])
 
         def gd_prep():
@@ -266,15 +288,10 @@ def tile_josephkalmanupdate_w_kernel(tc, s, z_bytes, z_scale, kgain, g, d, r, ou
             nc.vector.tensor_copy(out=dT[:].rearrange("p h T -> p T h"), in_=ps[:, :, 8:16])
             nc.vector.tensor_tensor(out=gdT[:], in0=gT[:], in1=dT[:], op=MULT)
 
-        def vplanes(u):
-            if u == 0:
-                return 2
-            if u == 1:
-                return 2
-            if u >= 34:
-                return 0
-            return 1 if u % 4 == 0 else 0
-
+        DSET = (2, 6)
+        esteps = [u for u in range(nu) if u % 8 not in DSET]
+        dunits = [u for u in range(nu) if u % 8 in DSET]
+        ns = len(esteps)
         tasks = {}
 
         def at(step, fn, *args):
@@ -286,77 +303,105 @@ def tile_josephkalmanupdate_w_kernel(tc, s, z_bytes, z_scale, kgain, g, d, r, ou
         at(2, k_turn, 3)
         at(2, gd_prep)
         at(3, k_q, 0)
-        at(4, k_q, 1)
-        at(5, kr_mul, 0)
-        at(6, kr_mul, 1)
-        at(7, kr_q, 0)
-        at(8, kr_q, 1)
-        at(8, q_all)
-        step0 = 0
+        at(3, k_q, 1)
+        at(4, kr_mul, 0)
+        at(4, kr_mul, 1)
+        at(5, kr_q, 0)
+        at(5, kr_q, 1)
+        at(5, q_all)
         for c, w in enumerate(CHUNKS):
-            end = 8 * (c + 1) - 1
+            end = 6 * (c + 1) - 1
             for h in range(w // 512):
-                at(end - 11 + h if c == len(CHUNKS) - 1 else end - 3 + h, s_perm, hh0(c) + h)
-                at(end - 10 + h if c == len(CHUNKS) - 1 else end - 2 + h, s_turn, hh0(c) + h)
+                at(end - 3 + h if c < len(CHUNKS) - 1 else end - 8, s_perm, hh0(c) + h)
+                at(end - 2 + h if c < len(CHUNKS) - 1 else end - 7, s_turn, hh0(c) + h)
             if c < len(CHUNKS) - 1:
                 k = end + 3
                 for h in range(w // 512):
-                    at(k + h, e_t1, c, h)
-                for h in range(w // 512):
-                    at(k + 2, e_mul, c, h, "w", gT)
-                for h in range(w // 512):
-                    at(k + 3, e_mul, c, h, "wd", gdT)
-                at(k + 3, e_q, c, "w")
-                at(k + 4, e_q, c, "wd")
-                at(k + 4, e_j, c)
+                    at(k, e_t1, c, h)
+                at(k + 1, e_mul, c, "w", gT)
+                at(k + 2, e_mul, c, "wd", gdT)
+                at(k + 2, e_q, c, "w")
+                at(k + 3, e_q, c, "wd")
+                at(k + 3, e_j, c)
 
         with tc.manual_schedule():
             nc.scalar.dma_start(out=zs[:], in_=z_scale.rearrange("(g p t) o -> p g (t o)", p=P, t=4))
-            load(0)
-            load(1)
+            order = []
+            for k in range(ns):
+                if k % 3 == 0:
+                    order += [esteps[k], dunits[k // 3]]
+                else:
+                    order += [esteps[k]]
+            nload = 0
+
+            load(order[0])
+            load(order[1])
+            load(order[2])
             nc.sync.dma_start(out=kg[:], in_=kgain)
             nc.gpsimd.memset(gdraw[:], 0.0)
             make_identity(nc, ident[:])
             nc.gpsimd.tensor_copy(out=identb[:], in_=ident[:])
-            load(2)
+            load(order[3])
             nc.sync.dma_start(out=rt[:], in_=r.rearrange("(g p t) -> p g t", p=P, t=4))
             nc.sync.dma_start(out=gdraw[0:8, :], in_=g.rearrange("(h x) -> h x", h=8))
             nc.sync.dma_start(out=gdraw[8:16, :], in_=d.rearrange("(h x) -> h x", h=8))
-            load(3)
+            load(order[4])
             nc.sync.dma_start(out=sraw[:], in_=s)
+            nload = 5
 
-            widen(0, vplanes(0))
-            widen(1, vplanes(1))
-            inter(0)
             last = len(CHUNKS) - 1
             fin = []
-            for u in range(nu):
-                if 4 <= u + 4 < nu:
-                    load(u + 4)
-                if u + 2 < nu:
-                    widen(u + 2, vplanes(u + 2))
-                if u + 1 < nu:
-                    inter(u + 1)
-                for fn, args in tasks.get(u, []):
-                    fn(*args)
+            done = {}
+
+            def quantized(u):
                 quant(u)
                 c, gp, lo, w = units[u]
+                done.setdefault(c, []).append(gp)
+                seq = done[c]
                 if c < last:
-                    if gp == KP - 1:
+                    if len(seq) == KP:
                         kzall(c)
                 else:
-                    if gp == 0:
+                    if len(seq) == 1:
                         for T in range(4):
                             fin.append(psum.tile([P, P], F32, name="tp", tag="tp", bufs=4))
                     for T in range(4):
-                        kzpass(c, 0, T, gp, fin[T][:])
+                        kzpass(c, 0, T, gp, fin[T][:], first=seq[0], final=gp if len(seq) == KP else -1)
+
+            for k in range(ns + 1):
+                while nload < len(order) and nload < k + k // 3 + 6:
+                    load(order[nload])
+                    nload += 1
+                if k < ns:
+                    widen_e(esteps[k])
+                if k >= 1:
+                    il_alloc(esteps[k - 1])
+                    word(esteps[k - 1], "S")
+                if k < ns:
+                    dd = dunits[k // 3]
+                    if k % 3 == 0:
+                        for t in range(3):
+                            d_widen(dd, t)
+                    elif k % 3 == 1:
+                        d_widen(dd, 3)
+                        d_inter(dd, 0)
+                        d_inter(dd, 1)
+                    else:
+                        d_inter(dd, 2)
+                        d_inter(dd, 3)
+                for fn, args in tasks.get(k, []):
+                    fn(*args)
+                if k >= 1 and k % 3 == 0:
+                    quantized(dunits[k // 3 - 1])
+                if k >= 1:
+                    quantized(esteps[k - 1])
             e_alloc(last)
             for T in range(4):
                 nc.vector.tensor_tensor(
                     out=ep[last]["t1"][:, 0, 128 * T : 128 * (T + 1)], in0=sT[:, 7, T, :], in1=fin[T][:], op=SUB
                 )
-            e_mul(last, 0, "wd", gdT)
-            e_mul(last, 0, "w", gT)
+            e_mul(last, "wd", gdT)
+            e_mul(last, "w", gT)
             e_q(last, "wd")
             e_q(last, "w")
             e_j(last)

@@ -26,7 +26,7 @@ def tile_josephkalmanupdate_w_kernel(tc, s, z_bytes, z_scale, kgain, g, d, r, ou
     nc = tc.nc
     with ExitStack() as ctx:
         keep = ctx.enter_context(tc.tile_pool(name="keep", bufs=1))
-        bpool = ctx.enter_context(tc.tile_pool(name="bpool", bufs=5))
+        bpool = ctx.enter_context(tc.tile_pool(name="bpool", bufs=6))
         work = ctx.enter_context(tc.tile_pool(name="work", bufs=3))
         cpool = ctx.enter_context(tc.tile_pool(name="cpool", bufs=2))
         epool = ctx.enter_context(tc.tile_pool(name="epool", bufs=2))
@@ -39,6 +39,7 @@ def tile_josephkalmanupdate_w_kernel(tc, s, z_bytes, z_scale, kgain, g, d, r, ou
                 units.append((c, gp, l0, w))
             l0 += w
         nu = len(units)
+        SPLIT = {}
 
         ident = keep.tile([P, P], F32, name="ident")
         identb = keep.tile([P, P], BF16, name="identb")
@@ -64,6 +65,7 @@ def tile_josephkalmanupdate_w_kernel(tc, s, z_bytes, z_scale, kgain, g, d, r, ou
 
         zb = {}
         planes = {}
+        pairs = {}
         il = {}
         codes = {}
         kz = {}
@@ -71,7 +73,7 @@ def tile_josephkalmanupdate_w_kernel(tc, s, z_bytes, z_scale, kgain, g, d, r, ou
 
         def load(u):
             c, gp, lo, w = units[u]
-            t_ = bpool.tile([P, 4, WMAX], U8, name="zb", tag="zb", bufs=5)
+            t_ = bpool.tile([P, 4, WMAX], U8, name="zb", tag="zb", bufs=6)
             nc.sync.dma_start(
                 out=t_[:, :, 0:w],
                 in_=z_bytes[512 * gp : 512 * (gp + 1), lo : lo + w].rearrange("(p t) w -> p t w", t=4),
@@ -80,12 +82,13 @@ def tile_josephkalmanupdate_w_kernel(tc, s, z_bytes, z_scale, kgain, g, d, r, ou
 
         def widen_e(u):
             c, gp, lo, w = units[u]
+            a0 = SPLIT.get(u, 0)
             p_ = work.tile([P, 2, WMAX * 2], BF16, name="pairs", tag="pairs", bufs=2, align_bytes=64)
-            planes[u] = p_
+            pairs[u] = p_
             for t in range(4):
                 nc.vector.tensor_scalar(
-                    out=p_[:, t // 2, 0 : 2 * w].rearrange("p (T A i e) -> p e A T i", T=4, i=4, e=2)[:, t % 2],
-                    in0=zb[u][:, t, 0:w].bitcast(F8).rearrange("p (A T i) -> p A T i", T=4, i=4),
+                    out=p_[:, t // 2, 32 * a0 : 2 * w].rearrange("p (l e) -> p e l", e=2)[:, t % 2],
+                    in0=zb[u][:, t, 16 * a0 : w].bitcast(F8),
                     scalar1=zs[:, gp, t : t + 1],
                     scalar2=None,
                     op0=MULT,
@@ -94,31 +97,52 @@ def tile_josephkalmanupdate_w_kernel(tc, s, z_bytes, z_scale, kgain, g, d, r, ou
         def il_alloc(u):
             il[u] = work.tile([P, 4 * WMAX], BF16, name="il", tag="il", bufs=4, align_bytes=64)
 
-        def word(u, eng, lo=0, hi=None):
+        def word(u, eng):
             c, gp, l_, w = units[u]
-            hi = w if hi is None else hi
+            a0 = SPLIT.get(u, 0)
             f = nc.scalar.copy if eng == "S" else nc.vector.tensor_copy
             f(
-                out=il[u][:, 4 * lo : 4 * hi].bitcast(F32).rearrange("p (c u) -> p c u", u=2),
-                in_=planes[u][:].rearrange("p u x -> p (u x)").bitcast(F32).rearrange("p (u c) -> p c u", u=2)[:, lo:hi, :],
+                out=il[u][:, 0 : 4 * w]
+                .bitcast(F32)
+                .rearrange("p (T A i u) -> p A T i u", T=4, i=4, u=2)[:, a0:],
+                in_=pairs[u][:]
+                .rearrange("p u x -> p (u x)")
+                .bitcast(F32)
+                .rearrange("p (u l) -> p l u", u=2)[:, 16 * a0 : w, :]
+                .rearrange("p (A T i) u -> p A T i u", T=4, i=4),
             )
 
         def d_widen(u, t):
             c, gp, lo, w = units[u]
+            n = 16 * SPLIT[u] if u in SPLIT else w
             if t == 0:
                 planes[u] = work.tile([P, 4, WMAX], BF16, name="planes", tag="planes", bufs=2, align_bytes=64)
             nc.scalar.activation(
-                out=planes[u][:, t, 0:w], in_=zb[u][:, t, 0:w].bitcast(F8), func=COPY, scale=zs[:, gp, t : t + 1]
+                out=planes[u][:, t, 0:n], in_=zb[u][:, t, 0:n].bitcast(F8), func=COPY, scale=zs[:, gp, t : t + 1]
             )
 
         def d_inter(u, T):
             c, gp, lo, w = units[u]
-            if T == 0:
-                il_alloc(u)
+            n = SPLIT[u] if u in SPLIT else w // 16
             nc.scalar.copy(
-                out=il[u][:, T * w : (T + 1) * w].rearrange("p (A i t) -> p A t i", i=4, t=4),
-                in_=planes[u][:, :, 0:w].rearrange("p t (A T i) -> p T A t i", T=4, i=4)[:, T],
+                out=il[u][:, T * w : T * w + 16 * n].rearrange("p (A i t) -> p A t i", i=4, t=4),
+                in_=planes[u][:, :, 0 : 16 * n].rearrange("p t (A T i) -> p T A t i", T=4, i=4)[:, T],
             )
+
+        def p_inter(u, b):
+            c, gp, lo, w = units[u]
+            ps = psum.tile([P, 2, 512], BF16, name="tp", tag="tp", bufs=4)
+            view = planes[u][:, :, 0:w].rearrange("p t (A T i) -> p T A i t", T=4, i=4)
+            for x in range(2):
+                j = 2 * b + x
+                nc.tensor.matmul(
+                    ps[:, x, :].rearrange("p (A i t) -> p A i t", i=4, t=4),
+                    lhsT=identb[:],
+                    rhs=view[:, j // 2, 32 * (j % 2) : 32 * (j % 2) + 32],
+                    start=True,
+                    stop=True,
+                )
+            nc.scalar.copy(out=il[u][:, 1024 * b : 1024 * (b + 1)], in_=ps[:].rearrange("p x n -> p (x n)"))
 
         def quant(u):
             c, gp, lo, w = units[u]
@@ -276,11 +300,13 @@ def tile_josephkalmanupdate_w_kernel(tc, s, z_bytes, z_scale, kgain, g, d, r, ou
                 nc.tensor.transpose(ps[:, T, :], sperm[q][:, T, :], identb[:])
             nc.scalar.copy(out=sT[:, q, :, :], in_=ps[:])
 
-        def gd_prep():
+        def gd_perm():
             nc.vector.tensor_copy(
                 out=gdperm[:].rearrange("p T (A i) -> p T A i", i=4),
                 in_=gdraw[:].rearrange("p (A T i) -> p T A i", T=4, i=4),
             )
+
+        def gd_prep():
             ps = psum.tile([P, 4, P], BF16, name="tp", tag="tp", bufs=4)
             for T in range(4):
                 nc.tensor.transpose(ps[:, T, :], gdperm[:, T, :], identb[:])
@@ -288,32 +314,36 @@ def tile_josephkalmanupdate_w_kernel(tc, s, z_bytes, z_scale, kgain, g, d, r, ou
             nc.vector.tensor_copy(out=dT[:].rearrange("p h T -> p T h"), in_=ps[:, :, 8:16])
             nc.vector.tensor_tensor(out=gdT[:], in0=gT[:], in1=dT[:], op=MULT)
 
-        DSET = (2, 6)
+        DSET = (1, 5)
         esteps = [u for u in range(nu) if u % 8 not in DSET]
         dunits = [u for u in range(nu) if u % 8 in DSET]
+        PSET = (13, 21, 29)
+        SPLIT.update({15: 24, 23: 24, 31: 24})
         ns = len(esteps)
         tasks = {}
 
         def at(step, fn, *args):
             tasks.setdefault(step, []).append((fn, args))
 
-        at(1, k_turn, 0)
-        at(1, k_turn, 1)
-        at(2, k_turn, 2)
-        at(2, k_turn, 3)
-        at(2, gd_prep)
-        at(3, k_q, 0)
-        at(3, k_q, 1)
-        at(4, kr_mul, 0)
-        at(4, kr_mul, 1)
-        at(5, kr_q, 0)
-        at(5, kr_q, 1)
-        at(5, q_all)
+        at(2, k_turn, 0)
+        at(2, k_turn, 1)
+        at(3, k_turn, 2)
+        at(3, k_turn, 3)
+        at(5, gd_perm)
+        at(6, gd_prep)
+        at(4, k_q, 0)
+        at(4, k_q, 1)
+        at(6, kr_mul, 0)
+        at(6, kr_mul, 1)
+        at(7, kr_q, 0)
+        at(7, kr_q, 1)
+        at(7, q_all)
         for c, w in enumerate(CHUNKS):
             end = 6 * (c + 1) - 1
             for h in range(w // 512):
-                at(end - 3 + h if c < len(CHUNKS) - 1 else end - 8, s_perm, hh0(c) + h)
-                at(end - 2 + h if c < len(CHUNKS) - 1 else end - 7, s_turn, hh0(c) + h)
+                k = 5 if c == 0 else end - 8 if c == len(CHUNKS) - 1 else end - 3 + h
+                at(k, s_perm, hh0(c) + h)
+                at(k + 1, s_turn, hh0(c) + h)
             if c < len(CHUNKS) - 1:
                 k = end + 3
                 for h in range(w // 512):
@@ -325,7 +355,9 @@ def tile_josephkalmanupdate_w_kernel(tc, s, z_bytes, z_scale, kgain, g, d, r, ou
                 at(k + 3, e_j, c)
 
         with tc.manual_schedule():
-            nc.scalar.dma_start(out=zs[:], in_=z_scale.rearrange("(g p t) o -> p g (t o)", p=P, t=4))
+            zsv = z_scale.rearrange("(g p t) o -> p g (t o)", p=P, t=4)
+            nc.scalar.dma_start(out=zs[:, 0:2, :], in_=zsv[:, 0:2, :])
+            nc.scalar.dma_start(out=zs[:, 2:8, :], in_=zsv[:, 2:8, :])
             order = []
             for k in range(ns):
                 if k % 3 == 0:
@@ -334,19 +366,36 @@ def tile_josephkalmanupdate_w_kernel(tc, s, z_bytes, z_scale, kgain, g, d, r, ou
                     order += [esteps[k]]
             nload = 0
 
-            load(order[0])
-            load(order[1])
-            load(order[2])
-            nc.sync.dma_start(out=kg[:], in_=kgain)
             nc.gpsimd.memset(gdraw[:], 0.0)
             make_identity(nc, ident[:])
             nc.gpsimd.tensor_copy(out=identb[:], in_=ident[:])
-            load(order[3])
-            nc.sync.dma_start(out=rt[:], in_=r.rearrange("(g p t) -> p g t", p=P, t=4))
-            nc.sync.dma_start(out=gdraw[0:8, :], in_=g.rearrange("(h x) -> h x", h=8))
-            nc.sync.dma_start(out=gdraw[8:16, :], in_=d.rearrange("(h x) -> h x", h=8))
-            load(order[4])
-            nc.sync.dma_start(out=sraw[:], in_=s)
+
+            def small():
+                nc.sync.dma_start(out=rt[:], in_=r.rearrange("(g p t) -> p g t", p=P, t=4))
+                nc.sync.dma_start(out=gdraw[0:8, :], in_=g.rearrange("(h x) -> h x", h=8))
+                nc.sync.dma_start(out=gdraw[8:16, :], in_=d.rearrange("(h x) -> h x", h=8))
+
+            def s_load(a, b):
+                nc.sync.dma_start(out=sraw[:, a:b], in_=s[:, a:b])
+
+            def k_load(a, b):
+                nc.sync.dma_start(out=kg[:, a:b], in_=kgain[:, a:b])
+
+            extra = {
+                4: [(k_load, (0, 2048))],
+                5: [(k_load, (2048, 4096))],
+                6: [(small, ())],
+                7: [(s_load, (0, 1536))],
+                9: [(s_load, (1536, 4096))],
+            }
+
+            def load_next(n):
+                load(order[n])
+                for fn, args in extra.get(n + 1, []):
+                    fn(*args)
+
+            for n in range(5):
+                load_next(n)
             nload = 5
 
             last = len(CHUNKS) - 1
@@ -370,25 +419,32 @@ def tile_josephkalmanupdate_w_kernel(tc, s, z_bytes, z_scale, kgain, g, d, r, ou
 
             for k in range(ns + 1):
                 while nload < len(order) and nload < k + k // 3 + 6:
-                    load(order[nload])
+                    load_next(nload)
                     nload += 1
                 if k < ns:
+                    il_alloc(esteps[k])
                     widen_e(esteps[k])
                 if k >= 1:
-                    il_alloc(esteps[k - 1])
-                    word(esteps[k - 1], "S")
+                    word(esteps[k - 1], "V" if k == ns else "S")
                 if k < ns:
                     dd = dunits[k // 3]
                     if k % 3 == 0:
-                        for t in range(3):
+                        il_alloc(dd)
+                        for t in range(4 if dd in PSET else 3):
                             d_widen(dd, t)
                     elif k % 3 == 1:
-                        d_widen(dd, 3)
-                        d_inter(dd, 0)
-                        d_inter(dd, 1)
+                        if dd not in PSET:
+                            d_widen(dd, 3)
+                        for x in (0, 1):
+                            p_inter(dd, x) if dd in PSET else d_inter(dd, x)
                     else:
-                        d_inter(dd, 2)
-                        d_inter(dd, 3)
+                        for x in (2, 3):
+                            p_inter(dd, x) if dd in PSET else d_inter(dd, x)
+                    if esteps[k] in SPLIT:
+                        for t in range(4):
+                            d_widen(esteps[k], t)
+                        for T in range(4):
+                            d_inter(esteps[k], T)
                 for fn, args in tasks.get(k, []):
                     fn(*args)
                 if k >= 1 and k % 3 == 0:

@@ -121,12 +121,22 @@ def tile_josephkalmanupdate_w_kernel(tc, s, z_bytes, z_scale, kgain, g, d, r, ou
                 out=planes[u][:, t, 0:n], in_=zb[u][:, t, 0:n].bitcast(F8), func=COPY, scale=zs[:, gp, t : t + 1]
             )
 
-        def d_inter(u, T):
+        def d_inter(u, b):
             c, gp, lo, w = units[u]
             n = SPLIT[u] if u in SPLIT else w // 16
+            if u in SPLIT:
+                if b:
+                    return
+                lo_a, hi_a = 0, n
+            else:
+                if b % 2:
+                    return
+                lo_a, hi_a = n * b // 4, n * (b + 2) // 4
             nc.scalar.copy(
-                out=il[u][:, T * w : T * w + 16 * n].rearrange("p (A i t) -> p A t i", i=4, t=4),
-                in_=planes[u][:, :, 0 : 16 * n].rearrange("p t (A T i) -> p T A t i", T=4, i=4)[:, T],
+                out=il[u][:, 0 : 4 * w].rearrange("p (T A i t) -> p A T i t", T=4, i=4, t=4)[:, lo_a:hi_a],
+                in_=planes[u][:, :, 0 : 16 * n]
+                .rearrange("p t l -> p l t")[:, 16 * lo_a : 16 * hi_a, :]
+                .rearrange("p (A T i) t -> p A T i t", T=4, i=4),
             )
 
         def p_inter(u, b):
@@ -318,7 +328,7 @@ def tile_josephkalmanupdate_w_kernel(tc, s, z_bytes, z_scale, kgain, g, d, r, ou
         esteps = [u for u in range(nu) if u % 8 not in DSET]
         dunits = [u for u in range(nu) if u % 8 in DSET]
         PSET = (13, 21, 29)
-        SPLIT.update({15: 24, 23: 24, 31: 24})
+        SPLIT.update({15: 16, 23: 16, 31: 16})
         ns = len(esteps)
         tasks = {}
 
@@ -345,7 +355,7 @@ def tile_josephkalmanupdate_w_kernel(tc, s, z_bytes, z_scale, kgain, g, d, r, ou
                 at(k, s_perm, hh0(c) + h)
                 at(k + 1, s_turn, hh0(c) + h)
             if c < len(CHUNKS) - 1:
-                k = end + 3
+                k = end + (5 if c == len(CHUNKS) - 2 else 4)
                 for h in range(w // 512):
                     at(k, e_t1, c, h)
                 at(k + 1, e_mul, c, "w", gT)
@@ -451,6 +461,9 @@ def tile_josephkalmanupdate_w_kernel(tc, s, z_bytes, z_scale, kgain, g, d, r, ou
                     quantized(dunits[k // 3 - 1])
                 if k >= 1:
                     quantized(esteps[k - 1])
+            for k in sorted(x for x in tasks if x > ns):
+                for fn, args in tasks[k]:
+                    fn(*args)
             e_alloc(last)
             for T in range(4):
                 nc.vector.tensor_tensor(

from contextlib import ExitStack

import concourse.mybir as mybir
from concourse.masks import make_identity

N, M, L = 128, 4096, 4096
FLOPS = 2 * N * M * L + 4 * N * N * L

F32 = mybir.dt.float32
BF16 = mybir.dt.bfloat16
U32 = mybir.dt.uint32
U8 = mybir.dt.uint8
F8 = mybir.dt.float8_e4m3fn
FP8X4 = mybir.dt.float8_e4m3fn_x4
MULT = mybir.AluOpType.mult
SUB = mybir.AluOpType.subtract
COPY = mybir.ActivationFunctionType.Copy

P = 128
KP = M // 512
CHUNKS = [512, 1024, 1024, 1024, 512]
WMAX = 1024


def tile_josephkalmanupdate_w_kernel(tc, s, z_bytes, z_scale, kgain, g, d, r, out):
    nc = tc.nc
    with ExitStack() as ctx:
        keep = ctx.enter_context(tc.tile_pool(name="keep", bufs=1))
        bpool = ctx.enter_context(tc.tile_pool(name="bpool", bufs=6))
        work = ctx.enter_context(tc.tile_pool(name="work", bufs=3))
        cpool = ctx.enter_context(tc.tile_pool(name="cpool", bufs=2))
        epool = ctx.enter_context(tc.tile_pool(name="epool", bufs=2))
        psum = ctx.enter_context(tc.psum_pool(name="psum", bufs=1))

        units = []
        l0 = 0
        for c, w in enumerate(CHUNKS):
            for gp in range(KP):
                units.append((c, gp, l0, w))
            l0 += w
        nu = len(units)
        SPLIT = {}

        ident = keep.tile([P, P], F32, name="ident")
        identb = keep.tile([P, P], BF16, name="identb")
        zs = keep.tile([P, KP, 4], F32, name="zs")
        rt = keep.tile([P, KP, 4], BF16, name="rt")
        gdraw = keep.tile([P, 512], BF16, name="gdraw")
        gdperm = keep.tile([P, 4, P], BF16, name="gdperm")
        gT = keep.tile([P, 8, 4], F32, name="gT")
        dT = keep.tile([P, 8, 4], F32, name="dT")
        gdT = keep.tile([P, 8, 4], F32, name="gdT")
        kg = keep.tile([P, M], BF16, name="kg")
        kT = keep.tile([P, KP, P * 4], BF16, name="kT", align_bytes=64)
        krT = keep.tile([P, KP, P * 4], BF16, name="krT", align_bytes=64)
        kq = keep.tile([P, KP, P], U32, name="kq", align_bytes=64)
        kqs = keep.tile([P, KP, P], U8, name="kqs", align_bytes=64)
        krq = keep.tile([P, KP, P], U32, name="krq", align_bytes=64)
        krqs = keep.tile([P, KP, P], U8, name="krqs", align_bytes=64)
        sraw = keep.tile([P, L], BF16, name="sraw")
        sperm = {}
        sT = keep.tile([P, 8, 4, P], BF16, name="sT")

        qj = psum.tile([P, P], F32, name="qj", tag="qj", bufs=1)

        zb = {}
        planes = {}
        pairs = {}
        il = {}
        codes = {}
        kz = {}
        ep = {}

        def load(u):
            c, gp, lo, w = units[u]
            t_ = bpool.tile([P, 4, WMAX], U8, name="zb", tag="zb", bufs=6)
            nc.sync.dma_start(
                out=t_[:, :, 0:w],
                in_=z_bytes[512 * gp : 512 * (gp + 1), lo : lo + w].rearrange("(p t) w -> p t w", t=4),
            )
            zb[u] = t_

        def widen_e(u):
            c, gp, lo, w = units[u]
            a0 = SPLIT.get(u, 0)
            p_ = work.tile([P, 2, WMAX * 2], BF16, name="pairs", tag="pairs", bufs=2, align_bytes=64)
            pairs[u] = p_
            for t in range(4):
                nc.vector.tensor_scalar(
                    out=p_[:, t // 2, 32 * a0 : 2 * w].rearrange("p (l e) -> p e l", e=2)[:, t % 2],
                    in0=zb[u][:, t, 16 * a0 : w].bitcast(F8),
                    scalar1=zs[:, gp, t : t + 1],
                    scalar2=None,
                    op0=MULT,
                )

        def il_alloc(u):
            il[u] = work.tile([P, 4 * WMAX], BF16, name="il", tag="il", bufs=4, align_bytes=64)

        def word(u, eng):
            c, gp, l_, w = units[u]
            a0 = SPLIT.get(u, 0)
            f = nc.scalar.copy if eng == "S" else nc.vector.tensor_copy
            f(
                out=il[u][:, 0 : 4 * w]
                .bitcast(F32)
                .rearrange("p (T A i u) -> p A T i u", T=4, i=4, u=2)[:, a0:],
                in_=pairs[u][:]
                .rearrange("p u x -> p (u x)")
                .bitcast(F32)
                .rearrange("p (u l) -> p l u", u=2)[:, 16 * a0 : w, :]
                .rearrange("p (A T i) u -> p A T i u", T=4, i=4),
            )

        def d_widen(u, t):
            c, gp, lo, w = units[u]
            n = 16 * SPLIT[u] if u in SPLIT else w
            if t == 0:
                planes[u] = work.tile([P, 4, WMAX], BF16, name="planes", tag="planes", bufs=2, align_bytes=64)
            nc.scalar.activation(
                out=planes[u][:, t, 0:n], in_=zb[u][:, t, 0:n].bitcast(F8), func=COPY, scale=zs[:, gp, t : t + 1]
            )

        def d_inter(u, b):
            c, gp, lo, w = units[u]
            n = SPLIT[u] if u in SPLIT else w // 16
            if u in SPLIT:
                if b:
                    return
                lo_a, hi_a = 0, n
            else:
                if b % 2:
                    return
                lo_a, hi_a = n * b // 4, n * (b + 2) // 4
            nc.scalar.copy(
                out=il[u][:, 0 : 4 * w].rearrange("p (T A i t) -> p A T i t", T=4, i=4, t=4)[:, lo_a:hi_a],
                in_=planes[u][:, :, 0 : 16 * n]
                .rearrange("p t l -> p l t")[:, 16 * lo_a : 16 * hi_a, :]
                .rearrange("p (A T i) t -> p A T i t", T=4, i=4),
            )

        def p_inter(u, b):
            c, gp, lo, w = units[u]
            ps = psum.tile([P, 2, 512], BF16, name="tp", tag="tp", bufs=4)
            view = planes[u][:, :, 0:w].rearrange("p t (A T i) -> p T A i t", T=4, i=4)
            for x in range(2):
                j = 2 * b + x
                nc.tensor.matmul(
                    ps[:, x, :].rearrange("p (A i t) -> p A i t", i=4, t=4),
                    lhsT=identb[:],
                    rhs=view[:, j // 2, 32 * (j % 2) : 32 * (j % 2) + 32],
                    start=True,
                    stop=True,
                )
            nc.scalar.copy(out=il[u][:, 1024 * b : 1024 * (b + 1)], in_=ps[:].rearrange("p x n -> p (x n)"))

        def quant(u):
            c, gp, lo, w = units[u]
            if c not in codes:
                codes[c] = (
                    cpool.tile([P, KP, WMAX], U32, name="zc", tag="zc", bufs=2, align_bytes=64),
                    cpool.tile([P, KP, WMAX], U8, name="zsc", tag="zsc", bufs=2, align_bytes=64),
                )
            cd, sc = codes[c]
            nc.vector.quantize_mx(
                out=cd[:, gp, 0:w].bitcast(FP8X4), scales=sc[:, gp, 0:w], in_=il[u][:, 0 : 4 * w]
            )

        def kzpass(c, h, T, gp, dst, first=0, final=KP - 1):
            cd, sc = codes[c]
            w = CHUNKS[c]
            c0 = T * (w // 4) + 128 * h
            nc.tensor.matmul_mx(
                out=dst,
                lhsT=cd[:, gp, c0 : c0 + 128].bitcast(FP8X4),
                lhsT_scale=sc[:, gp, c0 : c0 + 128],
                rhs=kq[:, gp, :].bitcast(FP8X4),
                rhs_scale=kqs[:, gp, :],
                start=(gp == first),
                stop=(gp == final),
            )

        def kzall(c):
            for h in range(CHUNKS[c] // 512):
                b_ = psum.tile([P, 4, P], F32, name="kz", tag="kz", bufs=3)
                kz[(c, h)] = b_
                for T in range(4):
                    for gp in range(KP):
                        kzpass(c, h, T, gp, b_[:, T, :])

        def hh0(c):
            return sum(CHUNKS[:c]) // 512

        def e_alloc(c):
            nh = CHUNKS[c] // 512
            ep[c] = dict(
                t1=epool.tile([P, 2, 512], F32, name="t1", tag="t1", bufs=1),
                w=epool.tile([P, 2, 512], BF16, name="w", tag="w", bufs=1, align_bytes=64),
                wd=epool.tile([P, 2, 512], BF16, name="wd", tag="wd", bufs=1, align_bytes=64),
                wq=epool.tile([P, 2, P], U32, name="wq", tag="wq", bufs=2, align_bytes=64),
                wqs=epool.tile([P, 2, P], U8, name="wqs", tag="wqs", bufs=2, align_bytes=64),
                wdq=epool.tile([P, 2, P], U32, name="wdq", tag="wdq", bufs=2, align_bytes=64),
                wdqs=epool.tile([P, 2, P], U8, name="wdqs", tag="wdqs", bufs=2, align_bytes=64),
            )

        def e_t1(c, h):
            if h == 0:
                e_alloc(c)
            hh = hh0(c) + h
            nc.vector.tensor_tensor(
                out=ep[c]["t1"][:, h, :].rearrange("p (n T) -> p n T", T=4),
                in0=sT[:, hh, :, :].rearrange("p T n -> p n T"),
                in1=kz[(c, h)][:].rearrange("p T n -> p n T"),
                op=SUB,
            )

        def e_mul(c, key, gain):
            nh = CHUNKS[c] // 512
            nc.vector.tensor_tensor(
                out=ep[c][key][:, 0:nh, :].rearrange("p h (n T) -> p h n T", T=4),
                in0=ep[c]["t1"][:, 0:nh, :].rearrange("p h (T n) -> p h n T" if c == len(CHUNKS) - 1 else "p h (n T) -> p h n T", T=4),
                in1=gain[:, hh0(c) : hh0(c) + nh, :].unsqueeze(2).to_broadcast([P, nh, P, 4]),
                op=MULT,
            )

        def e_q(c, key):
            nh = CHUNKS[c] // 512
            e = ep[c]
            nc.vector.quantize_mx(
                out=e[key + "q"][:, 0:nh, :].rearrange("p h n -> p (h n)").bitcast(FP8X4),
                scales=e[key + "qs"][:, 0:nh, :].rearrange("p h n -> p (h n)"),
                in_=e[key][:, 0:nh, :].rearrange("p h x -> p (h x)"),
            )

        def e_j(c):
            e = ep[c]
            for h in range(CHUNKS[c] // 512):
                nc.tensor.matmul_mx(
                    out=qj[:],
                    lhsT=e["wdq"][:, h, :].bitcast(FP8X4),
                    lhsT_scale=e["wdqs"][:, h, :],
                    rhs=e["wq"][:, h, :].bitcast(FP8X4),
                    rhs_scale=e["wqs"][:, h, :],
                    start=False,
                    stop=(hh0(c) + h == 7),
                )

        def tp_f32():
            return psum.tile([P, 2, 2, P], F32, name="tp", tag="tp", bufs=4)

        def k_turn(q):
            ps = tp_f32()
            words = kg[:].bitcast(F32)
            for j in range(2):
                for u in range(2):
                    b0 = 256 * (2 * q + j)
                    nc.tensor.transpose(ps[:, j, u, :], words[:, b0 + u : b0 + 256 : 2], ident[:])
            nc.scalar.copy(
                out=kT[:, 2 * q : 2 * q + 2, :].bitcast(F32).rearrange("p j (n u) -> p j n u", u=2),
                in_=ps[:].rearrange("p j u n -> p j n u"),
            )

        def k_q(q):
            a, b = 4 * q, 4 * q + 4
            nc.vector.quantize_mx(
                out=kq[:, a:b, :].rearrange("p g n -> p (g n)").bitcast(FP8X4),
                scales=kqs[:, a:b, :].rearrange("p g n -> p (g n)"),
                in_=kT[:, a:b, :].rearrange("p g x -> p (g x)"),
            )

        def kr_mul(q):
            a, b = 4 * q, 4 * q + 4
            nc.vector.tensor_tensor(
                out=krT[:, a:b, :].rearrange("p g (n t) -> p g n t", t=4),
                in0=kT[:, a:b, :].rearrange("p g (n t) -> p g n t", t=4),
                in1=rt[:, a:b, :].unsqueeze(2).to_broadcast([P, 4, P, 4]),
                op=MULT,
            )

        def kr_q(q):
            a, b = 4 * q, 4 * q + 4
            nc.vector.quantize_mx(
                out=krq[:, a:b, :].rearrange("p g n -> p (g n)").bitcast(FP8X4),
                scales=krqs[:, a:b, :].rearrange("p g n -> p (g n)"),
                in_=krT[:, a:b, :].rearrange("p g x -> p (g x)"),
            )

        def q_all():
            for gp in range(KP):
                nc.tensor.matmul_mx(
                    out=qj[:],
                    lhsT=krq[:, gp, :].bitcast(FP8X4),
                    lhsT_scale=krqs[:, gp, :],
                    rhs=kq[:, gp, :].bitcast(FP8X4),
                    rhs_scale=kqs[:, gp, :],
                    start=(gp == 0),
                    stop=False,
                )

        def s_perm(q):
            sperm[q] = epool.tile([P, 4, P], BF16, name="sperm", tag="sperm", bufs=2)
            nc.scalar.copy(
                out=sperm[q][:].rearrange("p T (A i) -> p T A i", i=4),
                in_=sraw[:, 512 * q : 512 * (q + 1)].rearrange("p (A T i) -> p T A i", T=4, i=4),
            )

        def s_turn(q):
            ps = psum.tile([P, 4, P], BF16, name="tp", tag="tp", bufs=4)
            for T in range(4):
                nc.tensor.transpose(ps[:, T, :], sperm[q][:, T, :], identb[:])
            nc.scalar.copy(out=sT[:, q, :, :], in_=ps[:])

        def gd_perm():
            nc.vector.tensor_copy(
                out=gdperm[:].rearrange("p T (A i) -> p T A i", i=4),
                in_=gdraw[:].rearrange("p (A T i) -> p T A i", T=4, i=4),
            )

        def gd_prep():
            ps = psum.tile([P, 4, P], BF16, name="tp", tag="tp", bufs=4)
            for T in range(4):
                nc.tensor.transpose(ps[:, T, :], gdperm[:, T, :], identb[:])
            nc.vector.tensor_copy(out=gT[:].rearrange("p h T -> p T h"), in_=ps[:, :, 0:8])
            nc.vector.tensor_copy(out=dT[:].rearrange("p h T -> p T h"), in_=ps[:, :, 8:16])
            nc.vector.tensor_tensor(out=gdT[:], in0=gT[:], in1=dT[:], op=MULT)

        DSET = (1, 5)
        esteps = [u for u in range(nu) if u % 8 not in DSET]
        dunits = [u for u in range(nu) if u % 8 in DSET]
        PSET = (13, 21, 29)
        SPLIT.update({15: 16, 23: 16, 31: 16})
        ns = len(esteps)
        tasks = {}

        def at(step, fn, *args):
            tasks.setdefault(step, []).append((fn, args))

        at(2, k_turn, 0)
        at(2, k_turn, 1)
        at(3, k_turn, 2)
        at(3, k_turn, 3)
        at(5, gd_perm)
        at(6, gd_prep)
        at(4, k_q, 0)
        at(4, k_q, 1)
        at(6, kr_mul, 0)
        at(6, kr_mul, 1)
        at(7, kr_q, 0)
        at(7, kr_q, 1)
        at(7, q_all)
        for c, w in enumerate(CHUNKS):
            end = 6 * (c + 1) - 1
            for h in range(w // 512):
                k = 5 if c == 0 else end - 8 if c == len(CHUNKS) - 1 else end - 3 + h
                at(k, s_perm, hh0(c) + h)
                at(k + 1, s_turn, hh0(c) + h)
            if c < len(CHUNKS) - 1:
                k = end + (5 if c == len(CHUNKS) - 2 else 4)
                for h in range(w // 512):
                    at(k, e_t1, c, h)
                at(k + 1, e_mul, c, "w", gT)
                at(k + 2, e_mul, c, "wd", gdT)
                at(k + 2, e_q, c, "w")
                at(k + 3, e_q, c, "wd")
                at(k + 3, e_j, c)

        with tc.manual_schedule():
            zsv = z_scale.rearrange("(g p t) o -> p g (t o)", p=P, t=4)
            nc.scalar.dma_start(out=zs[:, 0:2, :], in_=zsv[:, 0:2, :])
            nc.scalar.dma_start(out=zs[:, 2:8, :], in_=zsv[:, 2:8, :])
            order = []
            for k in range(ns):
                if k % 3 == 0:
                    order += [esteps[k], dunits[k // 3]]
                else:
                    order += [esteps[k]]
            nload = 0

            nc.gpsimd.memset(gdraw[:], 0.0)
            make_identity(nc, ident[:])
            nc.gpsimd.tensor_copy(out=identb[:], in_=ident[:])

            def small():
                nc.sync.dma_start(out=rt[:], in_=r.rearrange("(g p t) -> p g t", p=P, t=4))
                nc.sync.dma_start(out=gdraw[0:8, :], in_=g.rearrange("(h x) -> h x", h=8))
                nc.sync.dma_start(out=gdraw[8:16, :], in_=d.rearrange("(h x) -> h x", h=8))

            def s_load(a, b):
                nc.sync.dma_start(out=sraw[:, a:b], in_=s[:, a:b])

            def k_load(a, b):
                nc.sync.dma_start(out=kg[:, a:b], in_=kgain[:, a:b])

            extra = {
                4: [(k_load, (0, 2048))],
                5: [(k_load, (2048, 4096))],
                6: [(small, ())],
                7: [(s_load, (0, 1536))],
                9: [(s_load, (1536, 4096))],
            }

            def load_next(n):
                load(order[n])
                for fn, args in extra.get(n + 1, []):
                    fn(*args)

            for n in range(5):
                load_next(n)
            nload = 5

            last = len(CHUNKS) - 1
            fin = []
            done = {}

            def quantized(u):
                quant(u)
                c, gp, lo, w = units[u]
                done.setdefault(c, []).append(gp)
                seq = done[c]
                if c < last:
                    if len(seq) == KP:
                        kzall(c)
                else:
                    if len(seq) == 1:
                        for T in range(4):
                            fin.append(psum.tile([P, P], F32, name="tp", tag="tp", bufs=4))
                    for T in range(4):
                        kzpass(c, 0, T, gp, fin[T][:], first=seq[0], final=gp if len(seq) == KP else -1)

            for k in range(ns + 1):
                while nload < len(order) and nload < k + k // 3 + 6:
                    load_next(nload)
                    nload += 1
                if k < ns:
                    il_alloc(esteps[k])
                    widen_e(esteps[k])
                if k >= 1:
                    word(esteps[k - 1], "V" if k == ns else "S")
                if k < ns:
                    dd = dunits[k // 3]
                    if k % 3 == 0:
                        il_alloc(dd)
                        for t in range(4 if dd in PSET else 3):
                            d_widen(dd, t)
                    elif k % 3 == 1:
                        if dd not in PSET:
                            d_widen(dd, 3)
                        for x in (0, 1):
                            p_inter(dd, x) if dd in PSET else d_inter(dd, x)
                    else:
                        for x in (2, 3):
                            p_inter(dd, x) if dd in PSET else d_inter(dd, x)
                    if esteps[k] in SPLIT:
                        for t in range(4):
                            d_widen(esteps[k], t)
                        for T in range(4):
                            d_inter(esteps[k], T)
                for fn, args in tasks.get(k, []):
                    fn(*args)
                if k >= 1 and k % 3 == 0:
                    quantized(dunits[k // 3 - 1])
                if k >= 1:
                    quantized(esteps[k - 1])
            for k in sorted(x for x in tasks if x > ns):
                for fn, args in tasks[k]:
                    fn(*args)
            e_alloc(last)
            for T in range(4):
                nc.vector.tensor_tensor(
                    out=ep[last]["t1"][:, 0, 128 * T : 128 * (T + 1)], in0=sT[:, 7, T, :], in1=fin[T][:], op=SUB
                )
            e_mul(last, "wd", gdT)
            e_mul(last, "w", gT)
            e_q(last, "wd")
            e_q(last, "w")
            e_j(last)
            res = epool.tile([P, P], F32, name="res", tag="res", bufs=1)
            nc.vector.tensor_copy(out=res[:], in_=qj[:])
            nc.sync.dma_start(out=out, in_=res[:])
